import numpy as np
CORES = [6,14,22,30,134,142,150,158,262,270,278,286,390,398,406,414]
N = 16
ROOT = 9
def setup_inputs(rng):
    return {"x": rng.standard_normal((N, 128, 64), dtype=np.float32)}
def reference(x):
    y = np.full((N, 128, N * 64), np.nan, x.dtype)
    y[ROOT] = np.concatenate(list(x), axis=1)
    return {"y": y}

@@ -1,0 +1,59 @@
+W = 64
+ROOT_RANK = 9
+
+SCRATCH = {
+    "land": ("sbuf", [128, 16 * W], "float32"),
+    "xs": ("dram", [128, W], "float32"),
+    "rl": ("dram", [128, W], "float32"),
+}
+SEMAPHORES = ["loaded", "sent", "hop", "arr_a", "arr_b", "arr_c", "stored"]
+
+
+def relay_of(src):
+    if src // 128 != 0:
+        return None
+    chip = (src % 128) // 8
+    if chip % 2 == 1:
+        return 128 + 8 + (0 if chip == 1 else 2)
+    return 3 * 128 + 8 * chip + 2
+
+
+def rank_program(g, core, T, topo):
+    cores = list(T.cores)
+    root = cores[ROOT_RANK]
+    sem = T.sem
+    rank = T.rank_of(core)
+
+    def send(dst, out, src_ap, rsem):
+        rid, pid = topo.addr(dst, core)
+        g.remote_dma(out, src_ap, rsem, sem.sent, pid, rid, topo.mask(core, dst))
+        g.wait_ge(sem.sent, 8)
+
+    if core == root:
+        n_a = sum(1 for c in cores if c // 256 == 1 and c != root)
+        n_b = sum(1 for c in cores if c // 128 == 1)
+        n_c = sum(1 for c in cores if c // 128 == 0)
+        g.sync.dma_start(T.land[:, W * rank:W * (rank + 1)], T.x[:]).then_inc(sem.arr_a, 16)
+        g.sync.wait_ge(sem.arr_c, 8 * n_c)
+        g.sync.dma_start(T.y[:, 0:4 * W], T.land[:, 0:4 * W]).then_inc(sem.stored, 16)
+        g.scalar.wait_ge(sem.arr_a, 16 + 8 * n_a)
+        g.scalar.dma_start(T.y[:, 8 * W:16 * W], T.land[:, 8 * W:16 * W]).then_inc(sem.stored, 16)
+        g.scalar.wait_ge(sem.arr_b, 8 * n_b)
+        g.scalar.dma_start(T.y[:, 4 * W:8 * W], T.land[:, 4 * W:8 * W]).then_inc(sem.stored, 16)
+        g.wait_ge(sem.stored, 48)
+        return
+
+    if rank is not None:
+        g.sync.dma_start(T.xs[:], T.x[:]).then_inc(sem.loaded, 16)
+        g.wait_ge(sem.loaded, 16)
+        rel = relay_of(core)
+        if rel is not None:
+            send(rel, T.rl[:], T.xs[:], sem.hop)
+        else:
+            send(root, T.land[:, W * rank:W * (rank + 1)], T.xs[:], sem.arr_a if core // 256 == 1 else sem.arr_b)
+        return
+
+    for j, c in enumerate(cores):
+        if relay_of(c) == core:
+            g.wait_ge(sem.hop, 8)
+            send(root, T.land[:, W * j:W * (j + 1)], T.rl[:], sem.arr_c)

@@ -8,14 +8,15 @@ SCRATCH = {
 }
 SEMAPHORES = ["loaded", "sent", "hop", "arr_a", "arr_b", "arr_c", "stored"]
 
+RELAY = {0: (3, 0, 2), 3: (3, 3, 2), 1: (1, 1, 0), 2: (1, 0, 2)}
+
 
 def relay_of(src):
-    if src // 128 != 0:
-        return None
-    chip = (src % 128) // 8
-    if chip % 2 == 1:
-        return 128 + 8 + (0 if chip == 1 else 2)
-    return 3 * 128 + 8 * chip + 2
+    host, chip = src // 128, (src % 128) // 8
+    if host == 0:
+        h, c, k = RELAY[chip]
+        return 128 * h + 8 * c + k
+    return None
 
 
 def rank_program(g, core, T, topo):
@@ -24,10 +25,13 @@ def rank_program(g, core, T, topo):
     sem = T.sem
     rank = T.rank_of(core)
 
+    def engines(src, dst):
+        return bin(topo.mask(src, dst)).count("1")
+
     def send(dst, out, src_ap, rsem):
         rid, pid = topo.addr(dst, core)
         g.remote_dma(out, src_ap, rsem, sem.sent, pid, rid, topo.mask(core, dst))
-        g.wait_ge(sem.sent, 8)
+        g.wait_ge(sem.sent, engines(core, dst))
 
     if core == root:
         n_a = sum(1 for c in cores if c // 256 == 1 and c != root)
@@ -43,6 +47,9 @@ def rank_program(g, core, T, topo):
         g.wait_ge(sem.stored, 48)
         return
 
+    def group(c):
+        return sem.arr_a if c // 256 == 1 else (sem.arr_b if c // 128 == 1 else sem.arr_c)
+
     if rank is not None:
         g.sync.dma_start(T.xs[:], T.x[:]).then_inc(sem.loaded, 16)
         g.wait_ge(sem.loaded, 16)
@@ -50,10 +57,10 @@ def rank_program(g, core, T, topo):
         if rel is not None:
             send(rel, T.rl[:], T.xs[:], sem.hop)
         else:
-            send(root, T.land[:, W * rank:W * (rank + 1)], T.xs[:], sem.arr_a if core // 256 == 1 else sem.arr_b)
+            send(root, T.land[:, W * rank:W * (rank + 1)], T.xs[:], group(core))
         return
 
     for j, c in enumerate(cores):
         if relay_of(c) == core:
-            g.wait_ge(sem.hop, 8)
-            send(root, T.land[:, W * j:W * (j + 1)], T.rl[:], sem.arr_c)
+            g.wait_ge(sem.hop, engines(c, core))
+            send(root, T.land[:, W * j:W * (j + 1)], T.rl[:], group(c))

W = 64
ROOT_RANK = 9

SCRATCH = {
    "land": ("sbuf", [128, 16 * W], "float32"),
    "xs": ("dram", [128, W], "float32"),
    "rl": ("dram", [128, W], "float32"),
}
SEMAPHORES = ["loaded", "sent", "hop", "arr_a", "arr_b", "arr_c", "stored"]

RELAY = {0: (3, 0, 2), 3: (3, 3, 2), 1: (1, 1, 0), 2: (1, 0, 2)}


def relay_of(src):
    host, chip = src // 128, (src % 128) // 8
    if host == 0:
        h, c, k = RELAY[chip]
        return 128 * h + 8 * c + k
    return None


def rank_program(g, core, T, topo):
    cores = list(T.cores)
    root = cores[ROOT_RANK]
    sem = T.sem
    rank = T.rank_of(core)

    def engines(src, dst):
        return bin(topo.mask(src, dst)).count("1")

    def send(dst, out, src_ap, rsem):
        rid, pid = topo.addr(dst, core)
        g.remote_dma(out, src_ap, rsem, sem.sent, pid, rid, topo.mask(core, dst))
        g.wait_ge(sem.sent, engines(core, dst))

    if core == root:
        n_a = sum(1 for c in cores if c // 256 == 1 and c != root)
        n_b = sum(1 for c in cores if c // 128 == 1)
        n_c = sum(1 for c in cores if c // 128 == 0)
        g.sync.dma_start(T.land[:, W * rank:W * (rank + 1)], T.x[:]).then_inc(sem.arr_a, 16)
        g.sync.wait_ge(sem.arr_c, 8 * n_c)
        g.sync.dma_start(T.y[:, 0:4 * W], T.land[:, 0:4 * W]).then_inc(sem.stored, 16)
        g.scalar.wait_ge(sem.arr_a, 16 + 8 * n_a)
        g.scalar.dma_start(T.y[:, 8 * W:16 * W], T.land[:, 8 * W:16 * W]).then_inc(sem.stored, 16)
        g.scalar.wait_ge(sem.arr_b, 8 * n_b)
        g.scalar.dma_start(T.y[:, 4 * W:8 * W], T.land[:, 4 * W:8 * W]).then_inc(sem.stored, 16)
        g.wait_ge(sem.stored, 48)
        return

    def group(c):
        return sem.arr_a if c // 256 == 1 else (sem.arr_b if c // 128 == 1 else sem.arr_c)

    if rank is not None:
        g.sync.dma_start(T.xs[:], T.x[:]).then_inc(sem.loaded, 16)
        g.wait_ge(sem.loaded, 16)
        rel = relay_of(core)
        if rel is not None:
            send(rel, T.rl[:], T.xs[:], sem.hop)
        else:
            send(root, T.land[:, W * rank:W * (rank + 1)], T.xs[:], group(core))
        return

    for j, c in enumerate(cores):
        if relay_of(c) == core:
            g.wait_ge(sem.hop, engines(c, core))
            send(root, T.land[:, W * j:W * (j + 1)], T.rl[:], group(c))
